import numpy as np
import ml_dtypes


def mxq(x, axis, fmt="e4m3"):
    dtype, down = {"e4m3": (ml_dtypes.float8_e4m3fn, 7), "e5m2": (ml_dtypes.float8_e5m2, 14)}[fmt]
    v = np.moveaxis(np.asarray(x, np.float32).astype(ml_dtypes.bfloat16).astype(np.float64), axis, -1)
    blocks = v.reshape(v.shape[:-1] + (-1, 32))
    amax = np.abs(blocks).max(-1, keepdims=True)
    byte = np.maximum(np.where(amax > 0, np.frexp(amax)[1] - 1 + 127, 0) - down, 1)
    scale = np.exp2(byte - 127.0)
    codes = (blocks / scale).astype(np.float32).astype(dtype).astype(np.float64)
    return np.moveaxis((codes * scale).reshape(v.shape), -1, axis)


WIDE = False


def mx_kscale(k):
    if not WIDE:
        return np.ones(k)
    levels = np.array([10, -10, 5, -5, 0])
    if k % 512:
        return np.exp2(np.random.permutation(np.resize(levels, k // 32))).repeat(32)
    a = np.empty((k // 512, 16))
    for p in range(k // 512):
        a[p, :8] = np.random.permutation(np.resize(levels, 8))
        for g in range(8):
            far = levels[np.abs(levels - a[p, g]) >= 10]
            a[p, g + 8] = far[np.random.randint(len(far))]
    return np.exp2(a.ravel()).repeat(32)


def f64(x):
    return np.asarray(x).astype(np.float64)


def striped(idx):
    return np.tile(np.asarray(idx).reshape(-1, 16).T, (8, 1)).astype(np.uint16)


def unstriped(offs):
    return offs[:16].T.reshape(-1).astype(np.int64)


E2M1 = np.array([0.0, 0.5, 1.0, 1.5, 2.0, 3.0, 4.0, 6.0, -0.0, -0.5, -1.0, -1.5, -2.0, -3.0, -4.0, -6.0])


def pack_weight(w, fmt):
    k, n = w.shape
    w = f64(np.asarray(w, np.float32).astype(ml_dtypes.bfloat16)).reshape(k // 32, 32, n)
    amax = np.abs(w).max(1)
    if fmt == "e4m3":
        byte = np.frexp(amax)[1] - 1 + 127 - 7
    else:
        mant, ex = np.frexp(amax / 6.0)
        byte = np.where(mant > 0.5, ex, ex - 1) + 127
    byte = np.clip(np.where(amax > 0, byte, 1), 1, 254)
    scaled = (w * np.exp2(127.0 - byte)[:, None, :]).reshape(k, n).astype(np.float32)
    by_word = np.ascontiguousarray(scaled.reshape(k // 512, 128, 4, n).transpose(0, 1, 3, 2))
    if fmt == "e4m3":
        words = by_word.astype(ml_dtypes.float8_e4m3fn).view(np.uint8)
    else:
        c = by_word.astype(ml_dtypes.float4_e2m1fn).view(np.uint8) & 0xF
        words = (c[..., 0::2] | (c[..., 1::2] << 4)).reshape(k // 512, 128, 2 * n)
    return np.ascontiguousarray(words), np.ascontiguousarray(byte.astype(np.uint8).reshape(k // 512, 16, n))


def unpack_weight(words, scales, fmt):
    g, _, n = scales.shape
    words = np.ascontiguousarray(words).reshape(g, 128, n, -1)
    if fmt == "e4m3":
        vals = words.view(ml_dtypes.float8_e4m3fn).astype(np.float64)
    else:
        nib = np.empty((g, 128, n, 4), np.uint8)
        nib[..., 0::2] = words & 0xF
        nib[..., 1::2] = words >> 4
        vals = E2M1[nib]
    vals = vals * np.repeat(np.exp2(scales.astype(np.float64) - 127.0), 8, axis=1)[..., None]
    return vals.transpose(0, 1, 3, 2).reshape(g * 512, n)


def bf(x):
    return np.asarray(x, np.float32).astype(ml_dtypes.bfloat16)


def planes(Y):
    r, m = Y.shape
    b = f64(bf(Y)).reshape(r // 32, 32, m)
    amax = np.abs(b).max(1)
    byte = np.clip(np.where(amax > 0, np.frexp(amax)[1] - 1 + 127 - 7, 1), 1, 254)
    codes = (b * np.exp2(127.0 - byte)[:, None, :]).reshape(r, m).astype(np.float32).astype(ml_dtypes.float8_e4m3fn).view(np.uint8)
    words = codes.reshape(r // 512, 128, 4, m).transpose(0, 1, 3, 2)
    return np.ascontiguousarray(words), np.ascontiguousarray(byte.astype(np.uint8).reshape(r // 512, 16, m))


D, T, I, Q, E, X = 512, 2048, 512, 256, 512, 1024


def setup_inputs():
    n = np.random.standard_normal
    idx = np.random.permutation(T)[:I]
    idx2 = np.random.permutation(T)[:I]
    idx3 = np.random.permutation(X)[:I]
    fd = mx_kscale(D)
    fi = mx_kscale(I)
    keysp = pack_weight(n((D, T)) / fd[:, None], "e2m1")
    return {
        "query": (n((D, Q)) * 1.0 / np.sqrt(D) * fd[:, None]).astype(np.float32),
        "keys_words": keysp[0],
        "keys_scales": keysp[1],
        "os": (np.random.uniform(0.02, 0.08, (1, I)) * fi).astype(np.float32),
        "vals": (n((E, T))).astype(np.float32),
        "vals2": (n((E, X))).astype(np.float32),
        "vsc": (np.random.uniform(0.5, 2.0, (1, I)) / fi).astype(np.float32),
        "offs": striped(idx),
        "offs2": striped(idx2),
        "offs3": striped(idx3),
    }


def reference(query, keys_words, keys_scales, os, vals, vals2, vsc, offs, offs2, offs3):
    idx = unstriped(offs)
    idx2 = unstriped(offs2)
    idx3 = unstriped(offs3)
    keysu = unpack_weight(keys_words, keys_scales, "e2m1")
    queryq = mxq(f64(query), 0, "e4m3")
    a = queryq.T @ keysu
    w = a[:, idx] - a[:, idx2]
    wo1 = w * f64(os)
    wt1 = wo1.T
    vz = np.maximum(f64(vals)[:, idx], f64(vals2)[:, idx3]) * f64(vsc)
    vt1 = vz.T
    vt1q = mxq(vt1, 0, "e4m3")
    wt1q = mxq(wt1, 0, "e4m3")
    o = vt1q.T @ wt1q
    words, scales = planes(o)
    return o, words, scales

@@ -1,0 +1,234 @@
+from contextlib import ExitStack
+
+import concourse.mybir as mybir
+from concourse.masks import make_identity
+
+D, T, I, Q, E, X = 512, 2048, 512, 256, 512, 1024
+FLOPS = 2 * D * Q * T + 2 * I * E * Q
+
+F32 = mybir.dt.float32
+BF16 = mybir.dt.bfloat16
+I32 = mybir.dt.int32
+U32 = mybir.dt.uint32
+U16 = mybir.dt.uint16
+U8 = mybir.dt.uint8
+FP8X4 = mybir.dt.float8_e4m3fn_x4
+FP4X4 = mybir.dt.float4_e2m1fn_x4
+COPY = mybir.ActivationFunctionType.Copy
+MULT = mybir.AluOpType.mult
+MAX = mybir.AluOpType.max
+
+P = 128
+PACK = 4
+BANK = 512
+HALVES = Q // P
+
+
+def tile_attend_difference_mergedvalues_lean_pl_kernel(
+    tc, query, keys_words, keys_scales, w_factor, vals, vals2, v_factor, offs, offs2, offs3, out_0, out_1, out_2
+):
+    nc = tc.nc
+    with ExitStack() as ctx:
+        held = ctx.enter_context(tc.tile_pool(name="held", bufs=1))
+        psum = ctx.enter_context(tc.psum_pool(name="psum", bufs=1))
+
+        def sb(name, shape, dtype):
+            return held.tile(shape, dtype, name=name, align_bytes=64)
+
+        def bank(name):
+            return psum.tile([P, PACK, P], F32, name=name, tag="ring", bufs=6)
+
+        def gather_on_vector(out, window, offsets):
+            nc.vector.tensor_copy(out[:], window[:].indirect(offsets[:]))
+
+        def gather_on_scalar(out, window, offsets):
+            nc.scalar.activation(out[:], window[:].indirect(offsets[:]), COPY)
+
+        key_scales = sb("key_scales", [P, T], U8)
+        nc.vector.memset(key_scales[:].bitcast(I32), 0)
+
+        q_raw = sb("q_raw", [P, PACK, Q], F32)
+        nc.sync.dma_start(q_raw[:], query.rearrange("(p r) q -> p r q", r=PACK))
+        for quad in range(4):
+            nc.sync.dma_start(
+                key_scales[32 * quad : 32 * quad + 4, :].bitcast(I32),
+                keys_scales[0, 4 * quad : 4 * quad + 4, :].bitcast(I32),
+            )
+        key_words = sb("key_words", [P, 2 * T], U8)
+        nc.sync.dma_start(key_words[:].bitcast(I32), keys_words[0].bitcast(I32))
+
+        lists = []
+        for name, src in (("list1", offs), ("list2", offs2), ("list3", offs3)):
+            lists.append(held.tile([P, I // 16], U16, name=name))
+        list1, list2, list3 = lists
+
+        vals_rows = vals.rearrange("(p j) t -> j p t", j=PACK)
+        vals2_rows = vals2.rearrange("(p j) x -> j p x", j=PACK)
+        pool1 = [sb("pool1_%d" % j, [P, T], F32) for j in range(PACK)]
+        pool2 = [sb("pool2_%d" % j, [P, X], F32) for j in range(PACK)]
+        nc.sync.dma_start(pool1[0][:], vals_rows[0])
+        nc.sync.dma_start(list1[:], offs)
+        nc.sync.dma_start(list2[:], offs2)
+        nc.sync.dma_start(list3[:], offs3)
+        nc.sync.dma_start(pool2[0][:], vals2_rows[0])
+        for j in range(1, PACK):
+            nc.sync.dma_start(pool1[j][:], vals_rows[j])
+            nc.sync.dma_start(pool2[j][:], vals2_rows[j])
+
+        w_cols = sb("w_cols", [P, PACK], F32)
+        v_cols = sb("v_cols", [P, PACK], F32)
+        nc.gpsimd.dma_start(w_cols[:], w_factor.rearrange("o (p r) -> p (o r)", r=PACK))
+        nc.gpsimd.dma_start(v_cols[:], v_factor.rearrange("o (p r) -> p (o r)", r=PACK))
+        w_spread = w_cols[:].unsqueeze(1).to_broadcast([P, P, PACK])
+        v_spread = v_cols[:].unsqueeze(1).to_broadcast([P, P, PACK])
+
+        ident = sb("ident", [P, P], F32)
+        make_identity(nc, ident[:])
+
+        q_bf = sb("q_bf", [P, Q, PACK], BF16)
+        nc.vector.tensor_copy(q_bf[:], q_raw[:].rearrange("p r q -> p q r"))
+        q_codes = sb("q_codes", [P, Q], U32)
+        q_scales = sb("q_scales", [P, Q], U8)
+        nc.vector.quantize_mx(
+            out=q_codes[:].bitcast(FP8X4), scales=q_scales[:], in_=q_bf[:].rearrange("p q r -> p (q r)")
+        )
+
+        scores = [sb("scores_%d" % h, [P, T], F32) for h in range(HALVES)]
+        for h in range(HALVES):
+            for n in range(T // BANK):
+                acc = bank("acc")
+                flat = acc[:].rearrange("p r c -> p (r c)")
+                nc.tensor.matmul_mx(
+                    out=flat,
+                    lhsT=q_codes[:, h * P : (h + 1) * P].bitcast(FP8X4),
+                    lhsT_scale=q_scales[:, h * P : (h + 1) * P],
+                    rhs=key_words[:, 2 * n * BANK : 2 * (n + 1) * BANK].bitcast(FP4X4),
+                    rhs_scale=key_scales[:, n * BANK : (n + 1) * BANK],
+                    start=True,
+                    stop=True,
+                )
+                dst = scores[h][:, n * BANK : (n + 1) * BANK]
+                if n % 2 == 0:
+                    nc.scalar.copy(dst, flat)
+                else:
+                    nc.vector.tensor_copy(dst, flat)
+
+        w_bf = sb("w_bf", [P, Q, PACK], BF16)
+        w_banks = []
+        for h in range(HALVES):
+            plus = sb("plus_%d" % h, [P, I], F32)
+            minus = sb("minus_%d" % h, [P, I], F32)
+            gather_on_vector(plus, scores[h], list1)
+            nc.scalar.activation(minus[:], scores[h][:].indirect(list2[:]), COPY, scale=-1.0)
+            turned = bank("w_turned")
+            for r in range(PACK):
+                nc.tensor.matmul(turned[:, r, :], plus[:, r:I:PACK], ident[:], start=True, stop=False, is_transpose=True)
+                nc.tensor.matmul(turned[:, r, :], minus[:, r:I:PACK], ident[:], start=False, stop=True, is_transpose=True)
+            w_banks.append(turned)
+        for h in range(HALVES):
+            nc.vector.tensor_tensor(
+                w_bf[:, h * P : (h + 1) * P, :], w_banks[h][:].rearrange("p r q -> p q r"), w_spread, MULT
+            )
+        w_codes = sb("w_codes", [P, Q], U32)
+        w_scales = sb("w_scales", [P, Q], U8)
+
+        first = [sb("first_%d" % j, [P, I], F32) for j in range(PACK)]
+        second = [sb("second_%d" % j, [P, I], F32) for j in range(PACK)]
+        larger = [sb("larger_%d" % j, [P, PACK, P], F32) for j in range(PACK)]
+        v_bf = [sb("v_bf_%d" % j, [P, P, PACK], BF16) for j in range(PACK)]
+        v_codes = [sb("v_codes_%d" % j, [P, P], U32) for j in range(PACK)]
+        v_scales = [sb("v_scales_%d" % j, [P, P], U8) for j in range(PACK)]
+        res = [psum.tile([P, PACK, P], F32, name="res_%d" % h) for h in range(HALVES)]
+        res_sb = [sb("res_sb_%d" % j, [P, Q], F32) for j in range(PACK)]
+        out_rows = out_0.rearrange("(p j) q -> j p q", j=PACK)
+
+        def look_up(j):
+            gather_on_scalar(first[j], pool1[j], list1)
+            if j % 2 == 0:
+                gather_on_scalar(second[j], pool2[j], list3)
+            else:
+                gather_on_vector(second[j], pool2[j], list3)
+
+        def merge(j):
+            nc.vector.tensor_tensor(
+                larger[j][:].rearrange("p r s -> p s r"),
+                first[j][:].rearrange("p (s r) -> p s r", r=PACK),
+                second[j][:].rearrange("p (s r) -> p s r", r=PACK),
+                MAX,
+            )
+            turned = bank("v_turned")
+            for r in range(PACK):
+                nc.tensor.transpose(turned[:, r, :], larger[j][:, r, :], ident[:])
+            return turned
+
+        def scale_values(j, turned):
+            nc.vector.tensor_tensor(v_bf[j][:], turned[:].rearrange("p r m -> p m r"), v_spread, MULT)
+
+        def quantise_values(j):
+            nc.vector.quantize_mx(
+                out=v_codes[j][:].bitcast(FP8X4), scales=v_scales[j][:], in_=v_bf[j][:].rearrange("p m r -> p (m r)")
+            )
+
+        def product(j):
+            for h in range(HALVES):
+                nc.tensor.matmul_mx(
+                    out=res[h][:, j, :],
+                    lhsT=v_codes[j][:].bitcast(FP8X4),
+                    lhsT_scale=v_scales[j][:],
+                    rhs=w_codes[:, h * P : (h + 1) * P].bitcast(FP8X4),
+                    rhs_scale=w_scales[:, h * P : (h + 1) * P],
+                    start=True,
+                    stop=True,
+                )
+
+        def hand_out(j):
+            for h in range(HALVES):
+                nc.scalar.copy(res_sb[j][:, h * P : (h + 1) * P], res[h][:, j, :])
+            nc.sync.dma_start(out_rows[j], res_sb[j][:])
+
+        look_up(0)
+        look_up(1)
+        nc.vector.quantize_mx(
+            out=w_codes[:].bitcast(FP8X4), scales=w_scales[:], in_=w_bf[:].rearrange("p q r -> p (q r)")
+        )
+        t0 = merge(0)
+        t1 = merge(1)
+        scale_values(0, t0)
+        scale_values(1, t1)
+        look_up(2)
+        quantise_values(0)
+        quantise_values(1)
+        t2 = merge(2)
+        product(0)
+        product(1)
+        scale_values(2, t2)
+        look_up(3)
+        quantise_values(2)
+        hand_out(0)
+        hand_out(1)
+        product(2)
+        hand_out(2)
+        t3 = merge(3)
+        scale_values(3, t3)
+        quantise_values(3)
+        product(3)
+
+        y_bf = [sb("y_bf_%d" % h, [P, P, PACK], BF16) for h in range(HALVES)]
+        y_codes = sb("y_codes", [P, Q], U32)
+        y_scales = sb("y_scales", [P, Q], U8)
+        nc.vector.tensor_copy(y_bf[0][:], res[0][:].rearrange("p j q -> p q j"))
+        nc.scalar.copy(y_bf[1][:], res[1][:].rearrange("p j q -> p q j"))
+        hand_out(3)
+        for h in range(HALVES):
+            nc.vector.quantize_mx(
+                out=y_codes[:, h * P : (h + 1) * P].bitcast(FP8X4),
+                scales=y_scales[:, h * P : (h + 1) * P],
+                in_=y_bf[h][:].rearrange("p q j -> p (q j)"),
+            )
+        nc.sync.dma_start(out_1[0].rearrange("p c r -> p (c r)").bitcast(I32), y_codes[:].bitcast(I32))
+        for quad in range(4):
+            queue = nc.scalar if quad % 2 else nc.sync
+            queue.dma_start(
+                out_2[0, 4 * quad : 4 * quad + 4, :].bitcast(I32),
+                y_scales[32 * quad : 32 * quad + 4, :].bitcast(I32),
+            )

@@ -16,6 +16,7 @@ FP8X4 = mybir.dt.float8_e4m3fn_x4
 FP4X4 = mybir.dt.float4_e2m1fn_x4
 COPY = mybir.ActivationFunctionType.Copy
 MULT = mybir.AluOpType.mult
+SUB = mybir.AluOpType.subtract
 MAX = mybir.AluOpType.max
 
 P = 128
@@ -33,10 +34,10 @@ def tile_attend_difference_mergedvalues_lean_pl_kernel(
         psum = ctx.enter_context(tc.psum_pool(name="psum", bufs=1))
 
         def sb(name, shape, dtype):
-            return held.tile(shape, dtype, name=name, align_bytes=64)
+            return held.tile(shape, dtype, name=name, tag=name, align_bytes=64)
 
-        def bank(name):
-            return psum.tile([P, PACK, P], F32, name=name, tag="ring", bufs=6)
+        def bank(name, number):
+            return psum.tile([P, PACK, P], F32, name=name, tag="bank_%d" % number)
 
         def gather_on_vector(out, window, offsets):
             nc.vector.tensor_copy(out[:], window[:].indirect(offsets[:]))
@@ -66,19 +67,21 @@ def tile_attend_difference_mergedvalues_lean_pl_kernel(
         vals2_rows = vals2.rearrange("(p j) x -> j p x", j=PACK)
         pool1 = [sb("pool1_%d" % j, [P, T], F32) for j in range(PACK)]
         pool2 = [sb("pool2_%d" % j, [P, X], F32) for j in range(PACK)]
-        nc.sync.dma_start(pool1[0][:], vals_rows[0])
-        nc.sync.dma_start(list1[:], offs)
-        nc.sync.dma_start(list2[:], offs2)
-        nc.sync.dma_start(list3[:], offs3)
-        nc.sync.dma_start(pool2[0][:], vals2_rows[0])
-        for j in range(1, PACK):
-            nc.sync.dma_start(pool1[j][:], vals_rows[j])
-            nc.sync.dma_start(pool2[j][:], vals2_rows[j])
-
         w_cols = sb("w_cols", [P, PACK], F32)
         v_cols = sb("v_cols", [P, PACK], F32)
-        nc.gpsimd.dma_start(w_cols[:], w_factor.rearrange("o (p r) -> p (o r)", r=PACK))
-        nc.gpsimd.dma_start(v_cols[:], v_factor.rearrange("o (p r) -> p (o r)", r=PACK))
+        nc.sync.dma_start(list3[:], offs3)
+        nc.sync.dma_start(pool2[0][:], vals2_rows[0])
+        nc.sync.dma_start(pool2[1][:], vals2_rows[1])
+        nc.sync.dma_start(list2[:], offs2)
+        nc.sync.dma_start(list1[:], offs)
+        nc.sync.dma_start(pool1[0][:], vals_rows[0])
+        nc.sync.dma_start(w_cols[:], w_factor.rearrange("o (p r) -> p (o r)", r=PACK))
+        nc.sync.dma_start(v_cols[:], v_factor.rearrange("o (p r) -> p (o r)", r=PACK))
+        nc.sync.dma_start(pool2[2][:], vals2_rows[2])
+        nc.sync.dma_start(pool1[1][:], vals_rows[1])
+        nc.sync.dma_start(pool2[3][:], vals2_rows[3])
+        nc.sync.dma_start(pool1[2][:], vals_rows[2])
+        nc.sync.dma_start(pool1[3][:], vals_rows[3])
         w_spread = w_cols[:].unsqueeze(1).to_broadcast([P, P, PACK])
         v_spread = v_cols[:].unsqueeze(1).to_broadcast([P, P, PACK])
 
@@ -94,60 +97,49 @@ def tile_attend_difference_mergedvalues_lean_pl_kernel(
         )
 
         scores = [sb("scores_%d" % h, [P, T], F32) for h in range(HALVES)]
-        for h in range(HALVES):
-            for n in range(T // BANK):
-                acc = bank("acc")
-                flat = acc[:].rearrange("p r c -> p (r c)")
-                nc.tensor.matmul_mx(
-                    out=flat,
-                    lhsT=q_codes[:, h * P : (h + 1) * P].bitcast(FP8X4),
-                    lhsT_scale=q_scales[:, h * P : (h + 1) * P],
-                    rhs=key_words[:, 2 * n * BANK : 2 * (n + 1) * BANK].bitcast(FP4X4),
-                    rhs_scale=key_scales[:, n * BANK : (n + 1) * BANK],
-                    start=True,
-                    stop=True,
-                )
-                dst = scores[h][:, n * BANK : (n + 1) * BANK]
-                if n % 2 == 0:
-                    nc.scalar.copy(dst, flat)
-                else:
-                    nc.vector.tensor_copy(dst, flat)
-
+        taken = [sb("taken_%d" % h, [P, I], F32) for h in range(HALVES)]
+        diff = [sb("diff_%d" % h, [P, I], F32) for h in range(HALVES)]
         w_bf = sb("w_bf", [P, Q, PACK], BF16)
-        w_banks = []
-        for h in range(HALVES):
-            plus = sb("plus_%d" % h, [P, I], F32)
-            minus = sb("minus_%d" % h, [P, I], F32)
-            gather_on_vector(plus, scores[h], list1)
-            nc.scalar.activation(minus[:], scores[h][:].indirect(list2[:]), COPY, scale=-1.0)
-            turned = bank("w_turned")
-            for r in range(PACK):
-                nc.tensor.matmul(turned[:, r, :], plus[:, r:I:PACK], ident[:], start=True, stop=False, is_transpose=True)
-                nc.tensor.matmul(turned[:, r, :], minus[:, r:I:PACK], ident[:], start=False, stop=True, is_transpose=True)
-            w_banks.append(turned)
-        for h in range(HALVES):
-            nc.vector.tensor_tensor(
-                w_bf[:, h * P : (h + 1) * P, :], w_banks[h][:].rearrange("p r q -> p q r"), w_spread, MULT
-            )
         w_codes = sb("w_codes", [P, Q], U32)
         w_scales = sb("w_scales", [P, Q], U8)
-
         first = [sb("first_%d" % j, [P, I], F32) for j in range(PACK)]
         second = [sb("second_%d" % j, [P, I], F32) for j in range(PACK)]
         larger = [sb("larger_%d" % j, [P, PACK, P], F32) for j in range(PACK)]
-        v_bf = [sb("v_bf_%d" % j, [P, P, PACK], BF16) for j in range(PACK)]
+        v_bf = {}
         v_codes = [sb("v_codes_%d" % j, [P, P], U32) for j in range(PACK)]
         v_scales = [sb("v_scales_%d" % j, [P, P], U8) for j in range(PACK)]
-        res = [psum.tile([P, PACK, P], F32, name="res_%d" % h) for h in range(HALVES)]
-        res_sb = [sb("res_sb_%d" % j, [P, Q], F32) for j in range(PACK)]
-        out_rows = out_0.rearrange("(p j) q -> j p q", j=PACK)
+        res = []
+        out_rows = out_0.rearrange("(p j) q -> p j q", j=PACK)
 
-        def look_up(j):
-            gather_on_scalar(first[j], pool1[j], list1)
-            if j % 2 == 0:
-                gather_on_scalar(second[j], pool2[j], list3)
+        def score(h, n, on_vector):
+            acc = bank("acc", (4 * h + n) % 6)
+            flat = acc[:].rearrange("p r c -> p (r c)")
+            nc.tensor.matmul_mx(
+                out=flat,
+                lhsT=q_codes[:, h * P : (h + 1) * P].bitcast(FP8X4),
+                lhsT_scale=q_scales[:, h * P : (h + 1) * P],
+                rhs=key_words[:, 2 * n * BANK : 2 * (n + 1) * BANK].bitcast(FP4X4),
+                rhs_scale=key_scales[:, n * BANK : (n + 1) * BANK],
+                start=True,
+                stop=True,
+            )
+            dst = scores[h][:, n * BANK : (n + 1) * BANK]
+            if on_vector:
+                nc.vector.tensor_copy(dst, flat)
             else:
-                gather_on_vector(second[j], pool2[j], list3)
+                nc.scalar.copy(dst, flat)
+
+        def subtract(h):
+            nc.vector.tensor_tensor(diff[h][:], scores[h][:].indirect(list1[:]), taken[h][:], SUB)
+            turned = bank("w_turned", 6 + h)
+            for r in range(PACK):
+                nc.tensor.transpose(turned[:, r, :], diff[h][:, r:I:PACK], ident[:])
+            return turned
+
+        def scale_weights(h, turned):
+            nc.vector.tensor_tensor(
+                w_bf[:, h * P : (h + 1) * P, :], turned[:].rearrange("p r q -> p q r"), w_spread, MULT
+            )
 
         def merge(j):
             nc.vector.tensor_tensor(
@@ -156,12 +148,13 @@ def tile_attend_difference_mergedvalues_lean_pl_kernel(
                 second[j][:].rearrange("p (s r) -> p s r", r=PACK),
                 MAX,
             )
-            turned = bank("v_turned")
+            turned = bank("v_turned", j)
             for r in range(PACK):
                 nc.tensor.transpose(turned[:, r, :], larger[j][:, r, :], ident[:])
             return turned
 
-        def scale_values(j, turned):
+        def scale_values(j, turned, tag):
+            v_bf[j] = held.tile([P, P, PACK], BF16, name="v_bf_%d" % j, tag=tag, align_bytes=64)
             nc.vector.tensor_tensor(v_bf[j][:], turned[:].rearrange("p r m -> p m r"), v_spread, MULT)
 
         def quantise_values(j):
@@ -181,36 +174,49 @@ def tile_attend_difference_mergedvalues_lean_pl_kernel(
                     stop=True,
                 )
 
-        def hand_out(j):
+        def hand_out(staged, lo, hi):
             for h in range(HALVES):
-                nc.scalar.copy(res_sb[j][:, h * P : (h + 1) * P], res[h][:, j, :])
-            nc.sync.dma_start(out_rows[j], res_sb[j][:])
+                nc.scalar.copy(staged[:, :, h * P : (h + 1) * P], res[h][:, lo:hi, :])
+            nc.sync.dma_start(out_rows[:, lo:hi, :], staged[:])
 
-        look_up(0)
-        look_up(1)
+        gather_on_vector(second[0], pool2[0], list3)
+        gather_on_vector(second[1], pool2[1], list3)
+        for h in range(HALVES):
+            for n in range(4):
+                score(h, n, False)
+        gather_on_vector(taken[0], scores[0], list2)
+        w0 = subtract(0)
+        gather_on_scalar(first[0], pool1[0], list1)
+        gather_on_scalar(taken[1], scores[1], list2)
+        t0 = merge(0)
+        scale_weights(0, w0)
+        w1 = subtract(1)
+        gather_on_scalar(second[2], pool2[2], list3)
+        gather_on_scalar(first[1], pool1[1], list1)
+        scale_values(0, t0, "v_bf_0")
+        scale_weights(1, w1)
+        quantise_values(0)
+        t1 = merge(1)
         nc.vector.quantize_mx(
             out=w_codes[:].bitcast(FP8X4), scales=w_scales[:], in_=w_bf[:].rearrange("p q r -> p (q r)")
         )
-        t0 = merge(0)
-        t1 = merge(1)
-        scale_values(0, t0)
-        scale_values(1, t1)
-        look_up(2)
-        quantise_values(0)
-        quantise_values(1)
+        gather_on_scalar(second[3], pool2[3], list3)
+        gather_on_scalar(first[2], pool1[2], list1)
+        scale_values(1, t1, "v_bf_1")
         t2 = merge(2)
+        quantise_values(1)
+        res.extend([bank("res_0", 1), bank("res_1", 0)])
         product(0)
         product(1)
-        scale_values(2, t2)
-        look_up(3)
-        quantise_values(2)
-        hand_out(0)
-        hand_out(1)
-        product(2)
-        hand_out(2)
+        gather_on_scalar(first[3], pool1[3], list1)
+        early = held.tile([P, 2, Q], F32, name="early", tag="pool1_3", align_bytes=64)
+        hand_out(early, 0, 2)
         t3 = merge(3)
-        scale_values(3, t3)
+        scale_values(2, t2, "second_3")
+        scale_values(3, t3, "v_bf_3")
+        quantise_values(2)
         quantise_values(3)
+        product(2)
         product(3)
 
         y_bf = [sb("y_bf_%d" % h, [P, P, PACK], BF16) for h in range(HALVES)]
@@ -218,7 +224,8 @@ def tile_attend_difference_mergedvalues_lean_pl_kernel(
         y_scales = sb("y_scales", [P, Q], U8)
         nc.vector.tensor_copy(y_bf[0][:], res[0][:].rearrange("p j q -> p q j"))
         nc.scalar.copy(y_bf[1][:], res[1][:].rearrange("p j q -> p q j"))
-        hand_out(3)
+        late = sb("late", [P, 2, Q], F32)
+        hand_out(late, 2, PACK)
         for h in range(HALVES):
             nc.vector.quantize_mx(
                 out=y_codes[:, h * P : (h + 1) * P].bitcast(FP8X4),

@@ -23,6 +23,10 @@ P = 128
 PACK = 4
 BANK = 512
 HALVES = Q // P
+QUADS = 4
+LIST_COLUMNS = I // 16
+RUN = 4
+SCORE_BANKS = 6
 
 
 def tile_attend_difference_mergedvalues_lean_pl_kernel(
@@ -33,8 +37,8 @@ def tile_attend_difference_mergedvalues_lean_pl_kernel(
         held = ctx.enter_context(tc.tile_pool(name="held", bufs=1))
         psum = ctx.enter_context(tc.psum_pool(name="psum", bufs=1))
 
-        def sb(name, shape, dtype):
-            return held.tile(shape, dtype, name=name, tag=name, align_bytes=64)
+        def sbuf(name, shape, dtype, in_place_of=None):
+            return held.tile(shape, dtype, name=name, tag=in_place_of or name, align_bytes=64)
 
         def bank(name, number):
             return psum.tile([P, PACK, P], F32, name=name, tag="bank_%d" % number)
@@ -45,136 +49,134 @@ def tile_attend_difference_mergedvalues_lean_pl_kernel(
         def gather_on_scalar(out, window, offsets):
             nc.scalar.activation(out[:], window[:].indirect(offsets[:]), COPY)
 
-        key_scales = sb("key_scales", [P, T], U8)
+        def quantise(codes, scales, words):
+            nc.vector.quantize_mx(out=codes.bitcast(FP8X4), scales=scales, in_=words.rearrange("p c r -> p (c r)"))
+
+        key_scales = sbuf("key_scales", [P, T], U8)
         nc.vector.memset(key_scales[:].bitcast(I32), 0)
 
-        q_raw = sb("q_raw", [P, PACK, Q], F32)
+        q_raw = sbuf("q_raw", [P, PACK, Q], F32)
         nc.sync.dma_start(q_raw[:], query.rearrange("(p r) q -> p r q", r=PACK))
-        for quad in range(4):
+        for quad in range(QUADS):
             nc.sync.dma_start(
                 key_scales[32 * quad : 32 * quad + 4, :].bitcast(I32),
                 keys_scales[0, 4 * quad : 4 * quad + 4, :].bitcast(I32),
             )
-        key_words = sb("key_words", [P, 2 * T], U8)
-        nc.sync.dma_start(key_words[:].bitcast(I32), keys_words[0].bitcast(I32))
-
-        lists = []
-        for name, src in (("list1", offs), ("list2", offs2), ("list3", offs3)):
-            lists.append(held.tile([P, I // 16], U16, name=name))
-        list1, list2, list3 = lists
-
+        list1 = held.tile([P, LIST_COLUMNS], U16, name="list1")
+        list2 = held.tile([P, LIST_COLUMNS], U16, name="list2")
+        list3 = held.tile([P, LIST_COLUMNS], U16, name="list3")
+        key_words = [sbuf("key_words_%d" % u, [P, T], U8) for u in range(2)]
         vals_rows = vals.rearrange("(p j) t -> j p t", j=PACK)
         vals2_rows = vals2.rearrange("(p j) x -> j p x", j=PACK)
-        pool1 = [sb("pool1_%d" % j, [P, T], F32) for j in range(PACK)]
-        pool2 = [sb("pool2_%d" % j, [P, X], F32) for j in range(PACK)]
-        w_cols = sb("w_cols", [P, PACK], F32)
-        v_cols = sb("v_cols", [P, PACK], F32)
+        pool1 = [sbuf("pool1_%d" % j, [P, T], F32) for j in range(PACK)]
+        pool2 = [sbuf("pool2_%d" % j, [P, X], F32) for j in range(PACK)]
+        w_cols = sbuf("w_cols", [P, PACK], F32)
+        v_cols = sbuf("v_cols", [P, PACK], F32)
         nc.sync.dma_start(list3[:], offs3)
+        nc.sync.dma_start(key_words[0][:].bitcast(I32), keys_words[0, :, 0:T].bitcast(I32))
         nc.sync.dma_start(pool2[0][:], vals2_rows[0])
-        nc.sync.dma_start(pool2[1][:], vals2_rows[1])
-        nc.sync.dma_start(list2[:], offs2)
+        nc.sync.dma_start(key_words[1][:].bitcast(I32), keys_words[0, :, T : 2 * T].bitcast(I32))
         nc.sync.dma_start(list1[:], offs)
+        nc.sync.dma_start(list2[:], offs2)
+        nc.sync.dma_start(pool2[1][:], vals2_rows[1])
         nc.sync.dma_start(pool1[0][:], vals_rows[0])
         nc.sync.dma_start(w_cols[:], w_factor.rearrange("o (p r) -> p (o r)", r=PACK))
         nc.sync.dma_start(v_cols[:], v_factor.rearrange("o (p r) -> p (o r)", r=PACK))
-        nc.sync.dma_start(pool2[2][:], vals2_rows[2])
-        nc.sync.dma_start(pool1[1][:], vals_rows[1])
-        nc.sync.dma_start(pool2[3][:], vals2_rows[3])
-        nc.sync.dma_start(pool1[2][:], vals_rows[2])
+        for j in (1, 2):
+            nc.sync.dma_start(pool2[j + 1][:], vals2_rows[j + 1])
+            nc.sync.dma_start(pool1[j][:], vals_rows[j])
         nc.sync.dma_start(pool1[3][:], vals_rows[3])
         w_spread = w_cols[:].unsqueeze(1).to_broadcast([P, P, PACK])
         v_spread = v_cols[:].unsqueeze(1).to_broadcast([P, P, PACK])
 
-        ident = sb("ident", [P, P], F32)
+        ident = sbuf("ident", [P, P], F32)
         make_identity(nc, ident[:])
 
-        q_bf = sb("q_bf", [P, Q, PACK], BF16)
-        nc.vector.tensor_copy(q_bf[:], q_raw[:].rearrange("p r q -> p q r"))
-        q_codes = sb("q_codes", [P, Q], U32)
-        q_scales = sb("q_scales", [P, Q], U8)
-        nc.vector.quantize_mx(
-            out=q_codes[:].bitcast(FP8X4), scales=q_scales[:], in_=q_bf[:].rearrange("p q r -> p (q r)")
-        )
+        q_bf = [sbuf("q_bf_%d" % h, [P, P, PACK], BF16) for h in range(HALVES)]
+        q_codes = [sbuf("q_codes_%d" % h, [P, P], U32) for h in range(HALVES)]
+        q_scales = [sbuf("q_scales_%d" % h, [P, P], U8) for h in range(HALVES)]
+        for h, copy in enumerate((nc.vector.tensor_copy, nc.scalar.copy)):
+            copy(
+                q_bf[h][:].rearrange("p (c n) r -> p c r n", n=RUN),
+                q_raw[:, :, h * P : (h + 1) * P].rearrange("p r (c n) -> p c r n", n=RUN),
+            )
+        for h in range(HALVES):
+            quantise(q_codes[h][:], q_scales[h][:], q_bf[h][:])
 
-        scores = [sb("scores_%d" % h, [P, T], F32) for h in range(HALVES)]
-        taken = [sb("taken_%d" % h, [P, I], F32) for h in range(HALVES)]
-        diff = [sb("diff_%d" % h, [P, I], F32) for h in range(HALVES)]
-        w_bf = sb("w_bf", [P, Q, PACK], BF16)
-        w_codes = sb("w_codes", [P, Q], U32)
-        w_scales = sb("w_scales", [P, Q], U8)
-        first = [sb("first_%d" % j, [P, I], F32) for j in range(PACK)]
-        second = [sb("second_%d" % j, [P, I], F32) for j in range(PACK)]
-        larger = [sb("larger_%d" % j, [P, PACK, P], F32) for j in range(PACK)]
+        scores = [sbuf("scores_%d" % h, [P, T], F32) for h in range(HALVES)]
+        taken = [sbuf("taken_%d" % h, [P, I], F32) for h in range(HALVES)]
+        diff = [sbuf("diff_%d" % h, [P, I], F32) for h in range(HALVES)]
+        w_bf = {}
+        w_codes = [sbuf("w_codes_%d" % h, [P, P], U32) for h in range(HALVES)]
+        w_scales = [sbuf("w_scales_%d" % h, [P, P], U8) for h in range(HALVES)]
+        first = {j: sbuf("first_%d" % j, [P, I], F32) for j in range(1, PACK)}
+        second = {j: sbuf("second_%d" % j, [P, I], F32) for j in range(PACK)}
         v_bf = {}
-        v_codes = [sb("v_codes_%d" % j, [P, P], U32) for j in range(PACK)]
-        v_scales = [sb("v_scales_%d" % j, [P, P], U8) for j in range(PACK)]
-        res = []
+        v_codes = [sbuf("v_codes_%d" % j, [P, P], U32) for j in range(PACK)]
+        v_scales = [sbuf("v_scales_%d" % j, [P, P], U8) for j in range(PACK)]
         out_rows = out_0.rearrange("(p j) q -> p j q", j=PACK)
 
-        def score(h, n, on_vector):
-            acc = bank("acc", (4 * h + n) % 6)
+        def score(h, n):
+            acc = bank("acc", (T // BANK * h + n) % SCORE_BANKS)
             flat = acc[:].rearrange("p r c -> p (r c)")
             nc.tensor.matmul_mx(
                 out=flat,
-                lhsT=q_codes[:, h * P : (h + 1) * P].bitcast(FP8X4),
-                lhsT_scale=q_scales[:, h * P : (h + 1) * P],
-                rhs=key_words[:, 2 * n * BANK : 2 * (n + 1) * BANK].bitcast(FP4X4),
+                lhsT=q_codes[h][:].bitcast(FP8X4),
+                lhsT_scale=q_scales[h][:],
+                rhs=key_words[n // 2][:, 2 * (n % 2) * BANK : 2 * (n % 2 + 1) * BANK].bitcast(FP4X4),
                 rhs_scale=key_scales[:, n * BANK : (n + 1) * BANK],
                 start=True,
                 stop=True,
             )
-            dst = scores[h][:, n * BANK : (n + 1) * BANK]
-            if on_vector:
-                nc.vector.tensor_copy(dst, flat)
-            else:
-                nc.scalar.copy(dst, flat)
+            nc.scalar.copy(scores[h][:, n * BANK : (n + 1) * BANK], flat)
 
         def subtract(h):
             nc.vector.tensor_tensor(diff[h][:], scores[h][:].indirect(list1[:]), taken[h][:], SUB)
-            turned = bank("w_turned", 6 + h)
+            turned = bank("w_turned", SCORE_BANKS + h)
             for r in range(PACK):
                 nc.tensor.transpose(turned[:, r, :], diff[h][:, r:I:PACK], ident[:])
             return turned
 
         def scale_weights(h, turned):
-            nc.vector.tensor_tensor(
-                w_bf[:, h * P : (h + 1) * P, :], turned[:].rearrange("p r q -> p q r"), w_spread, MULT
-            )
+            w_bf[h] = sbuf("w_bf_%d" % h, [P, P, PACK], BF16)
+            nc.vector.tensor_tensor(w_bf[h][:], turned[:].rearrange("p r q -> p q r"), w_spread, MULT)
+
+        def quantise_weights(h):
+            quantise(w_codes[h][:], w_scales[h][:], w_bf[h][:])
 
         def merge(j):
+            larger = sbuf("larger_%d" % j, [P, 2, P, 2], F32)
             nc.vector.tensor_tensor(
-                larger[j][:].rearrange("p r s -> p s r"),
-                first[j][:].rearrange("p (s r) -> p s r", r=PACK),
-                second[j][:].rearrange("p (s r) -> p s r", r=PACK),
+                larger[:].rearrange("p u s v -> p s u v"),
+                first[j][:].rearrange("p (s u v) -> p s u v", u=2, v=2),
+                second[j][:].rearrange("p (s u v) -> p s u v", u=2, v=2),
                 MAX,
             )
             turned = bank("v_turned", j)
             for r in range(PACK):
-                nc.tensor.transpose(turned[:, r, :], larger[j][:, r, :], ident[:])
+                nc.tensor.transpose(turned[:, r, :], larger[:, r // 2, :, r % 2], ident[:])
             return turned
 
-        def scale_values(j, turned, tag):
-            v_bf[j] = held.tile([P, P, PACK], BF16, name="v_bf_%d" % j, tag=tag, align_bytes=64)
+        def scale_values(j, turned, in_place_of=None):
+            v_bf[j] = sbuf("v_bf_%d" % j, [P, P, PACK], BF16, in_place_of)
             nc.vector.tensor_tensor(v_bf[j][:], turned[:].rearrange("p r m -> p m r"), v_spread, MULT)
 
         def quantise_values(j):
-            nc.vector.quantize_mx(
-                out=v_codes[j][:].bitcast(FP8X4), scales=v_scales[j][:], in_=v_bf[j][:].rearrange("p m r -> p (m r)")
-            )
+            quantise(v_codes[j][:], v_scales[j][:], v_bf[j][:])
 
-        def product(j):
+        def product(res, j):
             for h in range(HALVES):
                 nc.tensor.matmul_mx(
                     out=res[h][:, j, :],
                     lhsT=v_codes[j][:].bitcast(FP8X4),
                     lhsT_scale=v_scales[j][:],
-                    rhs=w_codes[:, h * P : (h + 1) * P].bitcast(FP8X4),
-                    rhs_scale=w_scales[:, h * P : (h + 1) * P],
+                    rhs=w_codes[h][:].bitcast(FP8X4),
+                    rhs_scale=w_scales[h][:],
                     start=True,
                     stop=True,
                 )
 
-        def hand_out(staged, lo, hi):
+        def hand_out(res, staged, lo, hi):
             for h in range(HALVES):
                 nc.scalar.copy(staged[:, :, h * P : (h + 1) * P], res[h][:, lo:hi, :])
             nc.sync.dma_start(out_rows[:, lo:hi, :], staged[:])
@@ -182,58 +184,54 @@ def tile_attend_difference_mergedvalues_lean_pl_kernel(
         gather_on_vector(second[0], pool2[0], list3)
         gather_on_vector(second[1], pool2[1], list3)
         for h in range(HALVES):
-            for n in range(4):
-                score(h, n, False)
+            for n in range(T // BANK):
+                score(h, n)
         gather_on_vector(taken[0], scores[0], list2)
-        w0 = subtract(0)
-        gather_on_scalar(first[0], pool1[0], list1)
+        w_turned_0 = subtract(0)
         gather_on_scalar(taken[1], scores[1], list2)
-        t0 = merge(0)
-        scale_weights(0, w0)
-        w1 = subtract(1)
-        gather_on_scalar(second[2], pool2[2], list3)
-        gather_on_scalar(first[1], pool1[1], list1)
-        scale_values(0, t0, "v_bf_0")
-        scale_weights(1, w1)
-        quantise_values(0)
-        t1 = merge(1)
-        nc.vector.quantize_mx(
-            out=w_codes[:].bitcast(FP8X4), scales=w_scales[:], in_=w_bf[:].rearrange("p q r -> p (q r)")
-        )
-        gather_on_scalar(second[3], pool2[3], list3)
-        gather_on_scalar(first[2], pool1[2], list1)
-        scale_values(1, t1, "v_bf_1")
-        t2 = merge(2)
-        quantise_values(1)
-        res.extend([bank("res_0", 1), bank("res_1", 0)])
-        product(0)
-        product(1)
+        first[0] = sbuf("first_0", [P, I], F32, "key_words_1")
+        gather_on_scalar(first[0], pool1[0], list1)
+        for j in (1, 2):
+            gather_on_scalar(second[j + 1], pool2[j + 1], list3)
+            gather_on_scalar(first[j], pool1[j], list1)
         gather_on_scalar(first[3], pool1[3], list1)
-        early = held.tile([P, 2, Q], F32, name="early", tag="pool1_3", align_bytes=64)
-        hand_out(early, 0, 2)
-        t3 = merge(3)
-        scale_values(2, t2, "second_3")
-        scale_values(3, t3, "v_bf_3")
-        quantise_values(2)
-        quantise_values(3)
-        product(2)
-        product(3)
 
-        y_bf = [sb("y_bf_%d" % h, [P, P, PACK], BF16) for h in range(HALVES)]
-        y_codes = sb("y_codes", [P, Q], U32)
-        y_scales = sb("y_scales", [P, Q], U8)
-        nc.vector.tensor_copy(y_bf[0][:], res[0][:].rearrange("p j q -> p q j"))
-        nc.scalar.copy(y_bf[1][:], res[1][:].rearrange("p j q -> p q j"))
-        late = sb("late", [P, 2, Q], F32)
-        hand_out(late, 2, PACK)
+        scale_weights(0, w_turned_0)
+        w_turned_1 = subtract(1)
+        v_turned_0 = merge(0)
+        scale_weights(1, w_turned_1)
+        quantise_weights(0)
+        quantise_weights(1)
+        v_turned_1 = merge(1)
+        scale_values(0, v_turned_0, "second_1")
+        quantise_values(0)
+        scale_values(1, v_turned_1)
+        quantise_values(1)
+        v_turned_2 = merge(2)
+        res = [bank("res_0", 1), bank("res_1", 0)]
+        product(res, 0)
+        product(res, 1)
+        early = sbuf("early", [P, 2, Q], F32, "pool1_3")
+        hand_out(res, early, 0, 2)
+        v_turned_3 = merge(3)
+        scale_values(2, v_turned_2, "second_3")
+        quantise_values(2)
+        scale_values(3, v_turned_3)
+        quantise_values(3)
+        product(res, 2)
+        product(res, 3)
+
+        y_bf = [sbuf("y_bf_%d" % h, [P, P, PACK], BF16) for h in range(HALVES)]
+        y_codes = sbuf("y_codes", [P, Q], U32)
+        y_scales = sbuf("y_scales", [P, Q], U8)
+        for h, copy in enumerate((nc.vector.tensor_copy, nc.scalar.copy)):
+            copy(y_bf[h][:], res[h][:].rearrange("p j q -> p q j"))
+        late = sbuf("late", [P, 2, Q], F32)
+        hand_out(res, late, 2, PACK)
         for h in range(HALVES):
-            nc.vector.quantize_mx(
-                out=y_codes[:, h * P : (h + 1) * P].bitcast(FP8X4),
-                scales=y_scales[:, h * P : (h + 1) * P],
-                in_=y_bf[h][:].rearrange("p q j -> p (q j)"),
-            )
+            quantise(y_codes[:, h * P : (h + 1) * P], y_scales[:, h * P : (h + 1) * P], y_bf[h][:])
         nc.sync.dma_start(out_1[0].rearrange("p c r -> p (c r)").bitcast(I32), y_codes[:].bitcast(I32))
-        for quad in range(4):
+        for quad in range(QUADS):
             queue = nc.scalar if quad % 2 else nc.sync
             queue.dma_start(
                 out_2[0, 4 * quad : 4 * quad + 4, :].bitcast(I32),

from contextlib import ExitStack

import concourse.mybir as mybir
from concourse.masks import make_identity

D, T, I, Q, E, X = 512, 2048, 512, 256, 512, 1024
FLOPS = 2 * D * Q * T + 2 * I * E * Q

F32 = mybir.dt.float32
BF16 = mybir.dt.bfloat16
I32 = mybir.dt.int32
U32 = mybir.dt.uint32
U16 = mybir.dt.uint16
U8 = mybir.dt.uint8
FP8X4 = mybir.dt.float8_e4m3fn_x4
FP4X4 = mybir.dt.float4_e2m1fn_x4
COPY = mybir.ActivationFunctionType.Copy
MULT = mybir.AluOpType.mult
SUB = mybir.AluOpType.subtract
MAX = mybir.AluOpType.max

P = 128
PACK = 4
BANK = 512
HALVES = Q // P
QUADS = 4
LIST_COLUMNS = I // 16
RUN = 4
SCORE_BANKS = 6


def tile_attend_difference_mergedvalues_lean_pl_kernel(
    tc, query, keys_words, keys_scales, w_factor, vals, vals2, v_factor, offs, offs2, offs3, out_0, out_1, out_2
):
    nc = tc.nc
    with ExitStack() as ctx:
        held = ctx.enter_context(tc.tile_pool(name="held", bufs=1))
        psum = ctx.enter_context(tc.psum_pool(name="psum", bufs=1))

        def sbuf(name, shape, dtype, in_place_of=None):
            return held.tile(shape, dtype, name=name, tag=in_place_of or name, align_bytes=64)

        def bank(name, number):
            return psum.tile([P, PACK, P], F32, name=name, tag="bank_%d" % number)

        def gather_on_vector(out, window, offsets):
            nc.vector.tensor_copy(out[:], window[:].indirect(offsets[:]))

        def gather_on_scalar(out, window, offsets):
            nc.scalar.activation(out[:], window[:].indirect(offsets[:]), COPY)

        def quantise(codes, scales, words):
            nc.vector.quantize_mx(out=codes.bitcast(FP8X4), scales=scales, in_=words.rearrange("p c r -> p (c r)"))

        key_scales = sbuf("key_scales", [P, T], U8)
        nc.vector.memset(key_scales[:].bitcast(I32), 0)

        q_raw = sbuf("q_raw", [P, PACK, Q], F32)
        nc.sync.dma_start(q_raw[:], query.rearrange("(p r) q -> p r q", r=PACK))
        for quad in range(QUADS):
            nc.sync.dma_start(
                key_scales[32 * quad : 32 * quad + 4, :].bitcast(I32),
                keys_scales[0, 4 * quad : 4 * quad + 4, :].bitcast(I32),
            )
        list1 = held.tile([P, LIST_COLUMNS], U16, name="list1")
        list2 = held.tile([P, LIST_COLUMNS], U16, name="list2")
        list3 = held.tile([P, LIST_COLUMNS], U16, name="list3")
        key_words = [sbuf("key_words_%d" % u, [P, T], U8) for u in range(2)]
        vals_rows = vals.rearrange("(p j) t -> j p t", j=PACK)
        vals2_rows = vals2.rearrange("(p j) x -> j p x", j=PACK)
        pool1 = [sbuf("pool1_%d" % j, [P, T], F32) for j in range(PACK)]
        pool2 = [sbuf("pool2_%d" % j, [P, X], F32) for j in range(PACK)]
        w_cols = sbuf("w_cols", [P, PACK], F32)
        v_cols = sbuf("v_cols", [P, PACK], F32)
        nc.sync.dma_start(list3[:], offs3)
        nc.sync.dma_start(key_words[0][:].bitcast(I32), keys_words[0, :, 0:T].bitcast(I32))
        nc.sync.dma_start(pool2[0][:], vals2_rows[0])
        nc.sync.dma_start(key_words[1][:].bitcast(I32), keys_words[0, :, T : 2 * T].bitcast(I32))
        nc.sync.dma_start(list1[:], offs)
        nc.sync.dma_start(list2[:], offs2)
        nc.sync.dma_start(pool2[1][:], vals2_rows[1])
        nc.sync.dma_start(pool1[0][:], vals_rows[0])
        nc.sync.dma_start(w_cols[:], w_factor.rearrange("o (p r) -> p (o r)", r=PACK))
        nc.sync.dma_start(v_cols[:], v_factor.rearrange("o (p r) -> p (o r)", r=PACK))
        for j in (1, 2):
            nc.sync.dma_start(pool2[j + 1][:], vals2_rows[j + 1])
            nc.sync.dma_start(pool1[j][:], vals_rows[j])
        nc.sync.dma_start(pool1[3][:], vals_rows[3])
        w_spread = w_cols[:].unsqueeze(1).to_broadcast([P, P, PACK])
        v_spread = v_cols[:].unsqueeze(1).to_broadcast([P, P, PACK])

        ident = sbuf("ident", [P, P], F32)
        make_identity(nc, ident[:])

        q_bf = [sbuf("q_bf_%d" % h, [P, P, PACK], BF16) for h in range(HALVES)]
        q_codes = [sbuf("q_codes_%d" % h, [P, P], U32) for h in range(HALVES)]
        q_scales = [sbuf("q_scales_%d" % h, [P, P], U8) for h in range(HALVES)]
        for h, copy in enumerate((nc.vector.tensor_copy, nc.scalar.copy)):
            copy(
                q_bf[h][:].rearrange("p (c n) r -> p c r n", n=RUN),
                q_raw[:, :, h * P : (h + 1) * P].rearrange("p r (c n) -> p c r n", n=RUN),
            )
        for h in range(HALVES):
            quantise(q_codes[h][:], q_scales[h][:], q_bf[h][:])

        scores = [sbuf("scores_%d" % h, [P, T], F32) for h in range(HALVES)]
        taken = [sbuf("taken_%d" % h, [P, I], F32) for h in range(HALVES)]
        diff = [sbuf("diff_%d" % h, [P, I], F32) for h in range(HALVES)]
        w_bf = {}
        w_codes = [sbuf("w_codes_%d" % h, [P, P], U32) for h in range(HALVES)]
        w_scales = [sbuf("w_scales_%d" % h, [P, P], U8) for h in range(HALVES)]
        first = {j: sbuf("first_%d" % j, [P, I], F32) for j in range(1, PACK)}
        second = {j: sbuf("second_%d" % j, [P, I], F32) for j in range(PACK)}
        v_bf = {}
        v_codes = [sbuf("v_codes_%d" % j, [P, P], U32) for j in range(PACK)]
        v_scales = [sbuf("v_scales_%d" % j, [P, P], U8) for j in range(PACK)]
        out_rows = out_0.rearrange("(p j) q -> p j q", j=PACK)

        def score(h, n):
            acc = bank("acc", (T // BANK * h + n) % SCORE_BANKS)
            flat = acc[:].rearrange("p r c -> p (r c)")
            nc.tensor.matmul_mx(
                out=flat,
                lhsT=q_codes[h][:].bitcast(FP8X4),
                lhsT_scale=q_scales[h][:],
                rhs=key_words[n // 2][:, 2 * (n % 2) * BANK : 2 * (n % 2 + 1) * BANK].bitcast(FP4X4),
                rhs_scale=key_scales[:, n * BANK : (n + 1) * BANK],
                start=True,
                stop=True,
            )
            nc.scalar.copy(scores[h][:, n * BANK : (n + 1) * BANK], flat)

        def subtract(h):
            nc.vector.tensor_tensor(diff[h][:], scores[h][:].indirect(list1[:]), taken[h][:], SUB)
            turned = bank("w_turned", SCORE_BANKS + h)
            for r in range(PACK):
                nc.tensor.transpose(turned[:, r, :], diff[h][:, r:I:PACK], ident[:])
            return turned

        def scale_weights(h, turned):
            w_bf[h] = sbuf("w_bf_%d" % h, [P, P, PACK], BF16)
            nc.vector.tensor_tensor(w_bf[h][:], turned[:].rearrange("p r q -> p q r"), w_spread, MULT)

        def quantise_weights(h):
            quantise(w_codes[h][:], w_scales[h][:], w_bf[h][:])

        def merge(j):
            larger = sbuf("larger_%d" % j, [P, 2, P, 2], F32)
            nc.vector.tensor_tensor(
                larger[:].rearrange("p u s v -> p s u v"),
                first[j][:].rearrange("p (s u v) -> p s u v", u=2, v=2),
                second[j][:].rearrange("p (s u v) -> p s u v", u=2, v=2),
                MAX,
            )
            turned = bank("v_turned", j)
            for r in range(PACK):
                nc.tensor.transpose(turned[:, r, :], larger[:, r // 2, :, r % 2], ident[:])
            return turned

        def scale_values(j, turned, in_place_of=None):
            v_bf[j] = sbuf("v_bf_%d" % j, [P, P, PACK], BF16, in_place_of)
            nc.vector.tensor_tensor(v_bf[j][:], turned[:].rearrange("p r m -> p m r"), v_spread, MULT)

        def quantise_values(j):
            quantise(v_codes[j][:], v_scales[j][:], v_bf[j][:])

        def product(res, j):
            for h in range(HALVES):
                nc.tensor.matmul_mx(
                    out=res[h][:, j, :],
                    lhsT=v_codes[j][:].bitcast(FP8X4),
                    lhsT_scale=v_scales[j][:],
                    rhs=w_codes[h][:].bitcast(FP8X4),
                    rhs_scale=w_scales[h][:],
                    start=True,
                    stop=True,
                )

        def hand_out(res, staged, lo, hi):
            for h in range(HALVES):
                nc.scalar.copy(staged[:, :, h * P : (h + 1) * P], res[h][:, lo:hi, :])
            nc.sync.dma_start(out_rows[:, lo:hi, :], staged[:])

        gather_on_vector(second[0], pool2[0], list3)
        gather_on_vector(second[1], pool2[1], list3)
        for h in range(HALVES):
            for n in range(T // BANK):
                score(h, n)
        gather_on_vector(taken[0], scores[0], list2)
        w_turned_0 = subtract(0)
        gather_on_scalar(taken[1], scores[1], list2)
        first[0] = sbuf("first_0", [P, I], F32, "key_words_1")
        gather_on_scalar(first[0], pool1[0], list1)
        for j in (1, 2):
            gather_on_scalar(second[j + 1], pool2[j + 1], list3)
            gather_on_scalar(first[j], pool1[j], list1)
        gather_on_scalar(first[3], pool1[3], list1)

        scale_weights(0, w_turned_0)
        w_turned_1 = subtract(1)
        v_turned_0 = merge(0)
        scale_weights(1, w_turned_1)
        quantise_weights(0)
        quantise_weights(1)
        v_turned_1 = merge(1)
        scale_values(0, v_turned_0, "second_1")
        quantise_values(0)
        scale_values(1, v_turned_1)
        quantise_values(1)
        v_turned_2 = merge(2)
        res = [bank("res_0", 1), bank("res_1", 0)]
        product(res, 0)
        product(res, 1)
        early = sbuf("early", [P, 2, Q], F32, "pool1_3")
        hand_out(res, early, 0, 2)
        v_turned_3 = merge(3)
        scale_values(2, v_turned_2, "second_3")
        quantise_values(2)
        scale_values(3, v_turned_3)
        quantise_values(3)
        product(res, 2)
        product(res, 3)

        y_bf = [sbuf("y_bf_%d" % h, [P, P, PACK], BF16) for h in range(HALVES)]
        y_codes = sbuf("y_codes", [P, Q], U32)
        y_scales = sbuf("y_scales", [P, Q], U8)
        for h, copy in enumerate((nc.vector.tensor_copy, nc.scalar.copy)):
            copy(y_bf[h][:], res[h][:].rearrange("p j q -> p q j"))
        late = sbuf("late", [P, 2, Q], F32)
        hand_out(res, late, 2, PACK)
        for h in range(HALVES):
            quantise(y_codes[:, h * P : (h + 1) * P], y_scales[:, h * P : (h + 1) * P], y_bf[h][:])
        nc.sync.dma_start(out_1[0].rearrange("p c r -> p (c r)").bitcast(I32), y_codes[:].bitcast(I32))
        for quad in range(QUADS):
            queue = nc.scalar if quad % 2 else nc.sync
            queue.dma_start(
                out_2[0, 4 * quad : 4 * quad + 4, :].bitcast(I32),
                y_scales[32 * quad : 32 * quad + 4, :].bitcast(I32),
            )
